import numpy as np, ml_dtypes
CORES = [24,25,26,27,28,29,30,31]
N = 8
BF = ml_dtypes.bfloat16
W, L, S, T, HS, AS = 4096, 256, 16, 2, 2, 2
def parts(rng):
    D = rng.integers(0, W, (N, 8, 16, W)); one = rng.integers(0, W, (N, 8, 1, W))
    D = np.where((rng.random((N, 8, 1, W)) < 0.5) & (rng.random(D.shape) < 0.5), one, D)
    D = np.where(rng.random(D.shape) < 0.25, S * rng.integers(0, L, D.shape) + rng.integers(0, T, D.shape), D)
    X = rng.integers(0, 256, (N, 8, 16, W)); th = rng.integers(1000, 1800, (N, 8, 16))
    n = np.array([1, 1, 2, 2, 4, 4, 16, 16])[np.argsort(rng.random((N, 8)), axis=1)]
    j = (np.arange(16)[None, None, :] % n[:, :, None])[..., None]
    ti = np.take_along_axis(np.argsort(rng.random((N, 8, 16, 16)), axis=-1)[..., :3], j, 2)
    sg = np.take_along_axis(2 * rng.integers(0, 2, (N, 8, 16, 3)) - 1, j, 2)
    return D, X, th, ti, sg
def pack(D, X, th, ti, sg):
    return {"dg": np.ascontiguousarray(D.reshape(N, 128, W)).astype(np.int32), "xv": np.ascontiguousarray(X.reshape(N, 128, W)).astype(np.float32).astype(BF),
            "th": np.ascontiguousarray(th.reshape(N, 128, 1)).astype(np.int32), "ti": np.ascontiguousarray(ti.reshape(N, 128, 3)).astype(np.int32), "sg": np.ascontiguousarray(sg.reshape(N, 128, 3)).astype(np.int32)}
def setup_inputs(rng):
    return pack(*parts(rng))
def setup_inputs_corners(rng):
    D, X, th, ti, sg = parts(rng); c = np.arange(W)[None, :]; base = int(rng.integers(0, N)); o = rng.permutation(8)
    th = rng.choice(np.array([0, 1, 1365, 4080, 4081, 4081]), th.shape)
    for q in range(N):
        for g in range(8):
            m = int(o[g])
            if m == 0: D[q, g] = c
            if m == 1: D[q, g] = rng.choice(np.array([0, W - 1]), (16, W))
            if m == 2: D[q, g] = (c + 1 + np.arange(16)[:, None]) % W; th[q, g] = 4081
            if m == 3: D[q, g] = S * rng.integers(0, L, (16, W)) + rng.integers(0, T, (16, W))
            if m == 4: D[q, g] = rng.integers(0, W, (1, W)); th[q, g] = 4081
            if m == 5: D[q, g] = (c - 1) % W; th[q, g] = 0
            if m == 6: D[q, g] = rng.integers(0, W // 2, (16, W)) + (W // 2) * int(rng.integers(0, 2)); th[q, g] = 4081
            if m == 7: th[q, g] = 4080
    k = rng.random((N, 8, 1, W)); X = np.where(k < 0.1, 0, np.where(k < 0.2, 255, X))
    for q in (base % N, (base + 1) % N):
        for t in range(T): X[q, :, :, t::S] = 255
    a = (base + 2) % N; b = (base + 3) % N
    sg[a, :, :, 0] = -sg[a, :, :, 1]; sg[b] = sg[b][:, :, :1]
    return pack(D, X, th, ti, sg)
def setup_inputs_ties(rng):
    D, X, th, ti, sg = parts(rng)
    pr = rng.integers(0, 256, (8, 16, 24))
    pr[..., 12:] = np.minimum(pr[..., :12] + (np.arange(16)[None, :, None] == rng.integers(0, 16, (8, 1, 12))), 255)
    X = np.take_along_axis(np.broadcast_to(pr, (N, 8, 16, 24)), rng.integers(0, 24, (N, 8, 1, W)), 3)
    dd = np.add.reduce(np.abs(pr[:, :, :, None] - pr[:, :, None, :]), axis=1)
    th = dd[np.arange(8)[None, :, None], rng.integers(0, 24, (N, 8, 16)), rng.integers(0, 24, (N, 8, 16))] + rng.integers(0, 2, (N, 8, 16))
    return pack(D, X, th, ti, sg)
def setup_inputs_spread(rng):
    D, X, th, ti, sg = parts(rng)
    X = np.minimum((np.exp2(8 * rng.random((N, 8, 1, W))) * rng.random(X.shape)).astype(np.int64), 255)
    e = rng.choice(np.array([1, 2, 4]), (N, 8, 16, 1)); u = rng.random(D.shape)
    D = np.minimum((W * np.where(e == 1, u, np.where(e == 2, u * u, u * u * u * u))).astype(np.int64), W - 1)
    D = np.where(rng.random((N, 8, 16, 1)) < 0.5, D, W - 1 - D)
    th = np.minimum(np.exp2(12 * rng.random(th.shape)).astype(np.int64), 4081)
    return pack(D, X, th, ti, sg)
def setup_inputs_ends(rng):
    D, X, th, ti, sg = parts(rng)
    k = rng.random((N, 8, 1, W)); D = np.where(k < 0.4, (W - 1) * rng.integers(0, 2, k.shape), np.where(k < 0.75, (W - 1) * rng.integers(0, 2, D.shape), D))
    k = rng.random((N, 8, 1, W)); X = 255 * np.where(k < 0.3, rng.integers(0, 2, k.shape), rng.integers(0, 2, X.shape))
    th = 4081 * rng.integers(0, 2, th.shape); th[:, 0, 0] = 0; th[:, 7, 15] = 4081
    low = np.zeros((N, 8, 16, 1), np.int64); mid = rng.integers(1, 15, (N, 8, 16, 1))
    low[:, 4] = 1; mid[:, 4] = rng.integers(2, 15, (N, 16, 1))
    mid[:, 7] = 1 + np.arange(16).reshape(16, 1) % 14
    ti = np.concatenate([low, np.full((N, 8, 16, 1), 15), mid], axis=-1)
    ti = np.take_along_axis(ti, np.argsort(rng.random(ti.shape), axis=-1), 3)
    for q in (N - 2, N - 1, 0):
        c = (W - 1) * rng.integers(0, 2, (8, 1, L)); z = 255 * rng.integers(0, 2, (8, 1, L))
        c[..., 0] = 0; c[..., 1] = W - 1; c[..., L - 1] = W - 1; z[..., 0] = 0; z[..., 1] = 0; z[..., L - 1] = 0
        far = ((c == 0) == (z == 255)) & (rng.random((8, 1, L)) < 0.5); far[..., 0] = False; far[..., L - 1] = False
        off = (rng.integers(0, 16, (8, 16, L)) >> (3 * rng.integers(0, 2, (8, 1, L)))) * far
        x = np.abs(z - off)
        if q == N - 2:
            u = rng.permutation(8 * (L - 2))[:19 + 2 * int(rng.integers(0, 50))]; a = u // (L - 2); i = 1 + u % (L - 2)
            h = 255 * rng.integers(0, 2, (len(u), 16)); h[:, :2] = 0; h[:, 15] = 255
            c[a, 0, i] = W - 1; x[a, :, i] = h
        D[q, :, :, 0::S] = c; X[q, :, :, 0::S] = x
    for q in (N - 2, N - 1, 0, 1):
        D[q, :, :, 0] = 0; D[q, :, :, W - 1] = W - 1; X[q, :, :, 0] = 0; X[q, :, :, W - 1] = 255
    for q in (N - 1, 0):
        sg[q] = sg[q][:, :, :1]; sg[q, :, 0] = 1; sg[q, :, 15] = -1
    sg[1, :, :, 0] = -sg[1, :, :, 1]
    return pack(D, X, th, ti, sg)
def check_inputs(d):
    bad = []
    for k, lo, hi in (("dg", 0, W - 1), ("xv", 0, 255), ("th", 0, 4081), ("ti", 0, 15), ("sg", -1, 1)):
        a = np.asarray(d[k]).astype(np.float64)
        if not (np.min(a) >= lo and np.max(a) <= hi): bad.append("range of " + k)
    a = np.asarray(d["xv"]).astype(np.float64)
    if not np.all(a == np.floor(a)): bad.append("whole numbers in xv")
    a = np.asarray(d["ti"])
    if np.any(a[..., 0] == a[..., 1]) or np.any(a[..., 0] == a[..., 2]) or np.any(a[..., 1] == a[..., 2]): bad.append("different rows in a triple of ti")
    if np.any(np.asarray(d["sg"]) == 0): bad.append("no zero in sg")
    return bad
def reference(dg, xv, th, ti, sg):
    D = dg.astype(np.int64).reshape(N, 8, 16, W); X = xv.astype(np.float32).astype(np.int32).reshape(N, 8, 16, W); H = th.astype(np.int64).reshape(N, 8, 16, 1)
    G = np.zeros((N, 8, 16, 16), np.int64); np.put_along_axis(G, ti.astype(np.int64).reshape(N, 8, 16, 3), sg.astype(np.int64).reshape(N, 8, 16, 3), 3)
    def dist(q, E, x):
        y = np.take_along_axis(X[q], E.reshape(8, 1, 16 * L), 2).reshape(8, 16, 16, L)
        return np.add.reduce(np.abs(y - x[:, :, None, :]), axis=1).astype(np.int64)
    for t in range(T):
        v = S * np.arange(L) + t; new = np.array(D); last = []
        for r in range(N):
            s = (r + 1 + t) % N; x = X[r][:, :, v]; E = D[r][:, :, v]; go = np.ones((8, 16, L), bool)
            for step in range(HS + AS):
                q = r if step < HS else s
                n = np.take_along_axis(D[q], E, 2)
                go = go & (dist(q, n, x) < H[q]); E = np.where(go, n, E)
            d = dist(s, E, x); b = np.where(np.take_along_axis(X[s], E, 2) > x, 1, -1)
            cyc = np.abs(np.matmul(G[s], b)) == 3
            charged = np.matmul(np.abs(G[s]).transpose(0, 2, 1), cyc.astype(np.int64)) > 0
            A = int(np.count_nonzero(np.any(cyc, axis=1)))
            keep = np.argmin(np.where(charged, d, 2 ** 20), axis=1)
            gone = charged & (np.arange(16)[None, :, None] != keep[:, None, :])
            new[r][:, :, v] = np.where(gone, (37 * E + d + A) & (W - 1), D[r][:, :, v]); last.append(E)
        D = new
    yd = np.concatenate([D[:, :, :, t::S] for t in range(T)], axis=3)
    return {"yd": yd.reshape(N, 128, T * L).astype(np.float32), "ye": np.stack(last).reshape(N, 128, L).astype(np.float32)}

import numpy as np
from concourse.mybir import AluOpType, ActivationFunctionType
import comms_topo

ALU = AluOpType
ACT = ActivationFunctionType
NR = 8
L = 64
LT = 128
SK = 0.7
PAD = 16
DW = PAD + 4096
SINK = -60000.0
BIG = 32768.0
NXV = 0
ND16, ND32, NDF = 2, 3, 4
NOISE, SEED = 2000.0, 8250
PATTERN = "1010" "1010" "1001" "1000" "1011" "0010" "1110" "0000"
C = 256 // L
H = 256 // LT
E = 16 * L
CY, GAM, PEC, VF, SF, WAKE, RL = 1.0, 1.5, 0.5, 60, 75, 80, 2500

SCRATCH, SEMAPHORES = {}, []
for _s in ("dgi 4096 int32", "Df 4112 float32", "Xt 4112 bfloat16", "B8 16 bfloat16", "ioS 128 float32", "DiagF 2048 float32",
           "DiagB 2048 bfloat16", "DistB 2048 bfloat16", "If 128 float32", "nI 128 bfloat16", "C8 128 bfloat16", "Pd 128 bfloat16", "BO 128 bfloat16",
           "BOa 128 float32", "BOb 128 float32", "o32 128 float32", "ones 128 bfloat16", "G0 128 float32", "G1 128 float32", "G2 128 float32",
           "Gm 128 bfloat16", "Ga 128 bfloat16", "GT 128 bfloat16", "kc 4 int32", "ki 8 int32", "kf 8 float32", "thi 1 int32", "tii 3 int32", "sgi 3 int32",
           "tf 8 float32", "sgf 4 float32", "cnt 4 float32", "COi 16 int32", "CO 16 uint16", "acc 8 float32", "Ac 4 float32", "junk 256 bfloat16",
           "F1 256 float32", "F3 256 float32", "F4 256 int32", "off2 256 uint16", "off4 256 uint16", "bsg 256 bfloat16", "sq 256 bfloat16",
           "chs 256 bfloat16", "KT 256 float32", "m1 128 float32", "m2 64 float32", "m3 32 float32", "goT 256 float32", "go 256 float32",
           "E37 256 float32", "W1 256 float32", "Wm 256 float32", "Rg 256 float32", "U1 256 int32", "U2 256 int32", "yds 512 float32",
           "E4r 256 int32", "yes 256 float32"):
    _n, _w, _d = _s.split()
    SCRATCH[_n] = ("sbuf", [128, int(_w)], _d)
for _h in range(H):
    SCRATCH["mt%d" % _h] = ("sbuf", [128, 16], "float32")
for _t in range(2):
    for _n, _d in (("xc", "bfloat16"), ("xs", "bfloat16"), ("F2s", "float32"), ("F2r", "float32"), ("Rs", "float32"), ("Rr", "float32"), ("off0", "uint16"), ("E4", "int32")):
        SCRATCH[_n + str(_t)] = ("sbuf", [128, 256], _d)
    for _n in ("XRh", "XRs"):
        SCRATCH[_n + str(_t)] = ("sbuf", [128, 4096], "bfloat16")
for _k in range(4):
    SCRATCH["n%d" % _k] = ("sbuf", [128, 256], "float32")
    SCRATCH["off1%d" % _k] = ("sbuf", [128, 256], "uint16")
    SCRATCH["pen%d" % _k] = ("sbuf", [128, 256], "bfloat16")
for _n, _k, _d in (("dh", ND16, "float16"), ("dw", ND32, "float32"), ("df", NDF, "bfloat16"), ("ab", NDF, "bfloat16")):
    for _i in range(_k):
        SCRATCH[_n + str(_i)] = ("sbuf", [128, E], _d)
for _k in range(2):
    SCRATCH["abv%d" % _k] = ("sbuf", [128, 16 * LT], "bfloat16")
for _k in range(8):
    SCRATCH["ps%d" % _k] = ("psum", [128, 512], "float32")
NP = 4
PW = 4096 // NP
SEMAPHORES += ["cv", "cs", "cp", "cg", "sent", "ldx", "ldt", "ldi", "lds", "sty0", "sty1", "ste", "rx0", "rx1", "rr0", "rr1", "re"]
SEMAPHORES += ["ld%d" % _k for _k in range(NP)] + ["rf%d%d" % (_t, _c) for _t in range(2) for _c in range(C)]
COUNTER = {"v": "cv", "s": "cs", "p": "cp", "g": "cg"}


def on_vector(t, step, c):
    return PATTERN[(t * 4 + step) * C + c] == "1"


def build():
    ops, acc, bank, rots = [], {}, {}, {}

    def op(q, emit, rd, wr, cost, n=1, lat=0, sem=None, after=()):
        i, deps = len(ops), {}
        for k in after:
            deps[k] = 1
        for (b, lo, hi) in rd:
            for (l2, h2, w, j) in acc.get(b, []):
                if w and l2 < hi and lo < h2:
                    deps[j] = 1
        for (b, lo, hi) in wr:
            for (l2, h2, w, j) in acc.get(b, []):
                if l2 < hi and lo < h2:
                    deps[j] = 1
        for (b, lo, hi) in wr:
            acc[b] = [x for x in acc.get(b, []) if not (lo <= x[0] and x[1] <= hi)] + [(lo, hi, 1, i)]
        for (b, lo, hi) in rd:
            acc.setdefault(b, []).append((lo, hi, 0, i))
        for b in {x[0]: 1 for x in list(rd) + list(wr) if x[0][:2] == "ps"}:
            e = bank.setdefault(b, {"q": None, "cur": [], "prev": []})
            if e["q"] != q:
                e["q"], e["prev"], e["cur"] = q, e["cur"], []
            for j in e["prev"]:
                deps[j] = 1
            e["cur"].append(i)
        deps.pop(i, None)
        ops.append({"q": q, "emit": emit, "deps": sorted(deps), "cost": cost, "n": n, "lat": lat, "sem": sem, "i": i})
        return i

    def rot(kind, n):
        rots[kind] = rots.get(kind, -1) + 1
        return kind + str(rots[kind] % n)

    def ap(T, r):
        if isinstance(r, tuple):
            return T[r[0]][:, r[1]:r[2]] if len(r) == 3 else T[r[0]][:, r[1]:r[2]:r[3]]
        return r

    def R(*rs):
        return [r[:3] for r in rs if isinstance(r, tuple)]

    vc = lambda n: VF + n * CY
    sc = lambda n: SF + n * CY

    def ts(out, i0, s1, o0, s2=None, o1=None):
        def emit(g, T, X):
            if o1 is None:
                return [g.vector.tensor_scalar(ap(T, out), ap(T, i0), ap(T, s1), None, o0)]
            return [g.vector.tensor_scalar(ap(T, out), ap(T, i0), ap(T, s1), ap(T, s2), o0, o1)]
        op("v", emit, R(i0, s1, s2), R(out), vc(out[2] - out[1]))

    def tt(out, i0, i1, o, k=1):
        op("v", lambda g, T, X: [g.vector.tensor_tensor(ap(T, out), ap(T, i0), ap(T, i1), o)], R(i0, i1), R(out), VF + k * CY * (out[2] - out[1]))

    def cp(out, i0, f=1.0):
        op("v", lambda g, T, X: [g.vector.tensor_copy(ap(T, out), ap(T, i0))], R(i0), R(out), VF + f * CY * (out[2] - out[1]))

    def act(out, i0, f, bias=0.0, scale=1.0, accum=None, cost=None):
        def emit(g, T, X):
            if accum is not None:
                return [g.scalar.activation(ap(T, out), ap(T, i0), f, bias=ap(T, bias), scale=scale, accum_out=ap(T, accum))]
            return [g.scalar.activation(ap(T, out), ap(T, i0), f, bias=ap(T, bias), scale=scale)]
        op("s", emit, R(i0, bias), R(out) + (R(accum) if accum is not None else []), cost or sc(out[2] - out[1]))

    def mem(name, lo, hi, val):
        op("v", lambda g, T, X: [g.vector.memset(T[name][:, lo:hi], val)], [], [(name, lo, hi)], VF + (hi - lo) * CY * (0.5 if SCRATCH[name][2] == "bfloat16" else 1.0))

    def mm(out, parts, cost, first=True, last=True):
        def emit(g, T, X):
            r = None
            for k, (a, b) in enumerate(parts):
                r = g.tensor.matmul(ap(T, out), ap(T, a), ap(T, b), first and k == 0, last and k == len(parts) - 1)
            return [r]
        seen = {}
        for a, b in parts:
            for x in (a, b):
                lo, hi = seen.get(x[0], (x[1], x[2]))
                seen[x[0]] = (min(lo, x[1]), max(hi, x[2]))
        op("p", emit, [(k, v[0], v[1]) for k, v in seen.items()], R(out), cost)

    def pe_set(sel, src, ps, lo):
        parts = [((sel, p * 128, p * 128 + 128), (src, p, E, 16)) for p in range(16)]
        mm((ps, lo, lo + L), parts, PEC * L * 16 * (4 if src[:2] == "dw" else 1) + 60)

    def send(way, t, out, a, b, src, sem):
        i = op("g", lambda g, T, X: X[way](t, out, a, b, src, sem), [(src, a, b)], [], 1000, n=0)
        op("r", None, [], [(out, a, b)], 0, sem=sem, lat=RL, after=(i,))

    op("y", lambda g, T, X: [g.sync.dma_start(T.thi[:], T.th[:])], [], [("thi", 0, 1)], 60, sem="ldt", lat=2500)
    op("y", lambda g, T, X: [g.sync.dma_start(T.tii[:], T.ti[:])], [], [("tii", 0, 3)], 60, sem="ldi", lat=2500)
    op("y", lambda g, T, X: [g.sync.dma_start(T.sgi[:], T.sg[:])], [], [("sgi", 0, 3)], 60, sem="lds", lat=2500)
    op("s", lambda g, T, X: [g.scalar.dma_start(T.Xt[:, PAD:DW], T.xv[:])], [], [("Xt", PAD, DW)], 60, sem="ldx", lat=5000)
    for k in range(NP):
        op("y", lambda g, T, X, a=k * PW: [g.sync.dma_start(T.dgi[:, a:a + PW], T.dg[:, a:a + PW])], [], [("dgi", k * PW, k * PW + PW)], 60, sem="ld%d" % k, lat=4000 + 1500 * k)

    def iota(name, n, pat, cm=0, flag=True):
        def emit(g, T, X):
            if flag:
                return [g.iota(T[name][:, 0:n], pat, 0, cm, allow_small_or_imprecise_dtypes=True)]
            return [g.iota(T[name][:, 0:n], pat, 0, cm)]
        op("g", emit, [], [(name, 0, n)], 130 + 2 * n * CY)
    iota("kc", 1, [[0, 1]], 1, False)
    iota("ioS", 128, [[1, 128]])
    iota("COi", 16, [[1, 16]], 0, False)

    def pick(out, src, pat, o, base, cm):
        op("g", lambda g, T, X: [g.affine_select(ap(T, out), ap(T, src), pat, o, 0.0, base, cm)], R(src), R(out), 170 + 16 * CY)
    mem("Df", 0, PAD, SINK)
    mem("Xt", 0, PAD, 0.0)
    mem("ones", 0, 128, 1.0)
    mem("DiagB", 0, 2048, 0.0)
    mem("DistB", 0, 2048, 0.0)
    mem("o32", 0, 128, 0.03125)
    b8 = ("B8", 0, 8)
    for p in range(16):
        pick(("DiagB", 129 * p, 129 * p + 113, 16), ("ones", 0, 8), [[-16, 8]], ALU.is_equal, -p, 1)
        if p == 3:
            pick(b8, ("ones", 0, 8), [[-16, 8]], ALU.is_ge, 0, 1)
            pick(b8, b8, [[16, 8]], ALU.is_ge, 15, -1)
    for p in range(16):
        act(("DistB", 129 * p, 129 * p + 113, 16), b8, ACT.Identity, cost=sc(8))
    part, row, grp, p32 = [("kf", k, k + 1) for k in range(4)]
    ts(("ki", 0, 1), ("kc", 0, 1), 15, ALU.bitwise_and)
    ts(("ki", 1, 2), ("kc", 0, 1), 112, ALU.bitwise_and)
    cp(part, ("kc", 0, 1))
    cp(("kf", 1, 3), ("ki", 0, 2))
    ts(p32, row, 0.03125, ALU.mult)
    cp(("CO", 0, 16), ("COi", 0, 16))
    act(("DiagF", 0, 2048), ("DiagB", 0, 2048), ACT.Identity)
    io = ("ioS", 0, 128)
    ts(("If", 0, 128), io, part, ALU.is_equal)
    ts(("nI", 0, 128), io, part, ALU.is_equal, -1.0, ALU.mult)
    cp(("tf", 0, 1), ("thi", 0, 1))
    ts(("tf", 1, 2), ("tf", 0, 1), -BIG, ALU.mult, BIG, ALU.add)
    cp(("tf", 2, 5), ("tii", 0, 3))
    ts(("tf", 5, 8), ("tf", 2, 5), grp, ALU.add)
    cp(("sgf", 0, 3), ("sgi", 0, 3))
    for t in range(2):
        cp(("xc%d" % t, 0, 256), ("Xt", PAD + t, DW, 16), 0.5)
        send("send", t, "xs%d" % t, 0, 256, "xc%d" % t, "rx%d" % t)
    for k in range(NP):
        cp(("Df", PAD + k * PW, PAD + k * PW + PW), ("dgi", k * PW, k * PW + PW))
    for p in range(16):
        o = ("XRh0", p, 4096 - 15 + p, 16)
        if p < NXV:
            op("v", lambda g, T, X, o=o: [g.vector.tensor_copy(ap(T, o), T.xc0[:])], [("xc0", 0, 256)], R(o), vc(128))
        else:
            op("s", lambda g, T, X, o=o: [g.scalar.activation(ap(T, o), T.xc0[:], ACT.Identity)], [("xc0", 0, 256)], R(o), sc(256))

    def spread(dst, src):
        for p in range(16):
            op("g", lambda g, T, X, p=p: [g.affine_select(T[dst][:, p::16], T[src][:], [[0, 256]], ALU.is_equal, 0.0, 0, 0)],
               [(src, 0, 256)], [(dst, p, 4096 - 15 + p)], 170 + 512 * CY)

    def lane(t, c):
        q = PAD + 16 * c * L + t
        return ("Df", q, q + 16 * (L - 1) + 1, 16)

    def dgather(t, step, off, c):
        ch = (c * L, c * L + L)
        ps, of = ("ps%d" % (c % 2), 0, L), (off,) + ch
        vec = on_vector(t, step, c)
        d = rot("dh", ND16) if vec else rot("dw", ND32)
        if vec:
            op("v", lambda g, T, X: [g.vector.tensor_scalar(T[d][:], T.Df[:, 0:DW].indirect(ap(T, of)), -2048.0, None, ALU.add)],
               [("Df", 0, DW), of], [(d, 0, E)], VF + E * GAM * CY)
        else:
            op("s", lambda g, T, X: [g.scalar.activation(T[d][:], T.Df[:, 0:DW].indirect(ap(T, of)), ACT.Copy)],
               [("Df", 0, DW), of], [(d, 0, E)], SF + E * GAM * CY)
        pe_set("DiagB" if vec else "DiagF", d, ps[0], 0)
        sh = 2048.0 if vec else 0.0
        ts(("off1%d" % step,) + ch, ps, sh + PAD, ALU.add)
        act(("n%d" % step,) + ch, ps, ACT.Identity, sh + 4096.0 * (step + 1))

    def xgather(off, xr, c, m=None):
        of, x = (off, c * L, c * L + L), (xr, c * E, c * E + E)
        d = rot("df", NDF)
        m = m or ("ab" + d[2:], 0, E)
        op("v", lambda g, T, X: [g.vector.tensor_tensor(T[d][:], T.Xt[:, 0:DW].indirect(ap(T, of)), ap(T, x), ALU.subtract)],
           [("Xt", 0, DW), of, x], [(d, 0, E)], VF + E * GAM * CY)
        act(m, (d, 0, E), ACT.Abs)
        return d, m

    def walk(t, step, xr, fin, fout, c):
        ch = (c * L, c * L + L)
        d, m = xgather("off1%d" % step, xr, c)
        ps, pk = ("ps%d" % (2 + c % 2), 0, L), ("ps%d" % (4 + c % 2), 0, L)
        pe_set("DistB", m[0], ps[0], 0)
        act(("pen%d" % step,) + ch, ps, ACT.Relu, ("tf", 1, 2), BIG)
        pens = ["pen%d" % k for k in range(step - step % 2, step + 1)]
        mm(pk, [(("If", 0, 128), ("n%d" % step,) + ch)] + [(("nI", 0, 128), (pn,) + ch) for pn in pens], PEC * L * 6 + 60)
        tt((fout,) + ch, lane(t, c) if fin is None else (fin,) + ch, pk, ALU.max)
        if step == 1:
            send("send", t, "F2r%d" % t, ch[0], ch[1], fout, "rf%d%d" % (t, c))

    def setup_ballot():
        s = lambda n: (n, 0, 128)
        ts(s("C8"), io, part, ALU.is_equal, -8192.0, ALU.mult)
        ts(s("Pd"), io, part, ALU.is_equal, p32, ALU.mult)
        ts(s("BOa"), io, grp, ALU.subtract, -7.5, ALU.add)
        act(s("BOb"), s("BOa"), ACT.Abs)
        ts(s("BO"), s("BOb"), 8.0, ALU.is_lt)
        for k in range(3):
            ts(s("G%d" % k), io, ("tf", 5 + k, 6 + k), ALU.is_equal, ("sgf", k, k + 1), ALU.mult)
        tt(s("G0"), s("G0"), s("G1"), ALU.add, 2)
        tt(s("Gm"), s("G0"), s("G2"), ALU.add, 2)
        act(s("Ga"), s("Gm"), ACT.Abs)
        mm(("ps6", 0, 128), [(s("Gm"), s("nI"))], 150)
        act(s("GT"), ("ps6", 0, 128), ACT.Identity)
        mm(("ps7", 0, 64), [(s("Ga"), ("ones", 0, 64))], 150)
        act(("cnt", 0, 1), ("ps7", 0, 1), ACT.Identity, -0.5, -1.0)

    def vote(t, xr, c):
        e4, ch = "E4%d" % t, (c * L, c * L + L)
        h = c * L // LT
        ts((e4,) + ch, ("F4",) + ch, 4095, ALU.bitwise_and)
        ts(("off4",) + ch, (e4,) + ch, float(PAD), ALU.add)
        z = 16 * (c * L - h * LT)
        d, m = xgather("off4", xr, c, ("abv%d" % (h % 2), z, z + E))
        pe_set("DiagB", d, "ps%d" % (6 + h % 2), c * L - h * LT)

    def ballot(t, h):
        e4, W = "E4%d" % t, (h * LT, h * LT + LT)
        A = W[0]
        pt, pd = "ps%d" % (6 + h % 2), ("ps%d" % (2 + h % 2), 0, LT)
        q = [(pt, k * LT, k * LT + LT) for k in range(4)]
        parts = [(("DistB", p * 128, p * 128 + 128), ("abv%d" % (h % 2), p, 16 * LT, 16)) for p in range(16)] + [(("Pd", 0, 128), ("ones", 0, LT))]
        mm(pd, parts, PEC * LT * 17 + 60, last=False)
        act(("bsg",) + W, q[0], ACT.Sign, -0.5)
        mm(q[1], [(("GT", 0, 128), ("bsg",) + W)], PEC * LT + 60)
        act(("sq",) + W, q[1], ACT.Square)
        mm(q[2], [(("Ga", 0, 128), ("sq",) + W)], PEC * LT + 60)
        mm(q[3], [(("BO", 0, 128), ("sq",) + W)], PEC * LT + 60)
        act(("chs",) + W, q[2], ACT.Sign, ("cnt", 0, 1))
        act(("junk",) + W, q[3], ACT.Sign, -16.5, 1.0, ("acc", h, h + 1))
        mm(pd, [(("C8", 0, 128), ("chs",) + W)], PEC * LT + 60, first=False)
        if h == H - 1:
            mm(("ps5", 0, 1), [(("o32", 0, 128), ("acc", k, k + 1)) for k in range(H)], 64 * 4 * PEC * H + 60)
            act(("Ac", 0, 1), ("ps5", 0, 1), ACT.Identity, 1024.0 - 4096.0)
        op("v", lambda g, T, X: [g.vector.transpose(ap(T, ("KT",) + W), ap(T, pd))], [pd], [("KT",) + W], vc(LT))
        ts(("E37",) + W, (e4,) + W, 37.0, ALU.mult, 262144.0, ALU.add)
        tt(("W1",) + W, ("E37",) + W, pd, ALU.add)
        tt(("Wm",) + W, ("W1",) + W, ("chs",) + W, ALU.mult, 2)
        src, s0, w = "KT", A, LT
        for dst in ("m1", "m2", "m3", "mt%d" % h):
            w = w // 2
            d0 = 0 if dst[:2] == "mt" else h * w
            tt((dst, d0, d0 + w), (src, s0, s0 + 2 * w, 2), (src, s0 + 1, s0 + 2 * w, 2), ALU.min, 2)
            src, s0 = dst, d0
        nb = LT // 16
        op("v", lambda g, T, X: [g.vector.tensor_tensor(ap(T, ("goT",) + W), T["mt%d" % h][:, 0:nb].indirect(T.CO[:, 0:nb]), ap(T, ("KT",) + W), ALU.is_lt)],
           [("mt%d" % h, 0, nb), ("CO", 0, 16), ("KT",) + W], [("goT",) + W], VF + LT * GAM * CY)
        op("v", lambda g, T, X: [g.vector.transpose(ap(T, ("go",) + W), ap(T, ("goT",) + W))], [("goT",) + W], [("go",) + W], vc(LT))
        tt(("Rg",) + W, ("Wm",) + W, ("go",) + W, ALU.mult, 2)

    def finish(t):
        al = (0, 256)
        rs, rr, Dt = ("Rs%d" % t,) + al, ("Rr%d" % t,) + al, ("Df", PAD + t, DW, 16)
        ts(rs, ("Rg",) + al, ("Ac", 0, 1), ALU.add)
        send("back", t, rr[0], 0, 256, rs[0], "rr%d" % t)
        tt(("U1",) + al, Dt, rr, ALU.max, 2)
        ts(("U2",) + al, ("U1",) + al, 4095, ALU.bitwise_and)
        y = ("yds", 256 * t, 256 * t + 256)
        if t == 0:
            cp(Dt, ("U2",) + al)
            act(y, Dt, ACT.Identity)
        else:
            cp(y, ("U2",) + al)
        op("y", lambda g, T, X: [g.sync.dma_start(T.yd[:, y[1]:y[2]], ap(T, y))], [y], [], 60, sem="sty%d" % t, lat=2500)

    def walked(t):
        al = (0, 256)
        send("back", t, "E4r", 0, 256, "E4%d" % t, "re")
        cp(("yes",) + al, ("E4r",) + al)
        op("y", lambda g, T, X: [g.sync.dma_start(T.ye[:], T["yes"][:])], [("yes",) + al], [], 60, sem="ste", lat=2500)

    for t in range(2):
        ts(("off0%d" % t, 0, 256), ("Df", PAD + t, DW, 16), float(PAD), ALU.add)
    spread("XRs0", "xs0")
    setup_ballot()
    for t in range(2):
        tasks = []
        f2, xh, xs = "F2r%d" % t, "XRh%d" % t, "XRs%d" % t
        for c in range(C):
            ch = (c * L, c * L + L)
            z = SK * c

            def take(c=c, ch=ch, f2=f2):
                ts(("off2",) + ch, (f2,) + ch, PAD - 8192.0, ALU.add)
            for st, fn, ar in ((0, dgather, (t, 0, "off0%d" % t, c)), (1.0, dgather, (t, 1, "off10", c)), (1.1, walk, (t, 0, xh, None, "F1", c)),
                               (2, walk, (t, 1, xh, "F1", "F2s%d" % t, c)), (3, take, ()), (3, dgather, (t, 2, "off2", c)),
                               (4, dgather, (t, 3, "off12", c)), (4.1, walk, (t, 2, xs, f2, "F3", c)), (5, walk, (t, 3, xs, "F3", "F4", c)), (6, vote, (t, xs, c))):
                tasks.append((st + z, len(tasks), fn, ar))
            if (c + 1) * L % LT == 0:
                tasks.append((6.2 + z, len(tasks), ballot, (t, c * L // LT)))
        for _a, _b, fn, ar in sorted(tasks, key=lambda x: x[:2]):
            fn(*ar)
        if t == 1:
            walked(t)
        finish(t)
        if t == 0:
            spread("XRh1", "xc1")
            spread("XRs1", "xs1")
    return ops


def schedule(ops):
    n = len(ops)
    rnd = np.random.RandomState(SEED).rand(n)
    succ = [[] for _ in range(n)]
    for o in ops:
        for d in o["deps"]:
            succ[d].append(o["i"])
    prio = [0.0] * n
    for i in range(n - 1, -1, -1):
        prio[i] = ops[i]["cost"] + ops[i]["lat"] + max([prio[j] + WAKE for j in succ[i]] + [0.0])
    prio = [prio[i] + NOISE * float(rnd[i]) for i in range(n)]
    left = [len(o["deps"]) for o in ops]
    ready_at = [0.0] * n
    ready = [i for i in range(n) if left[i] == 0]
    free, order, fin = {}, [], [0.0] * n
    while ready:
        best = None
        for i in ready:
            q = ops[i]["q"]
            st = ready_at[i] if q == "r" else max(ready_at[i], free.get(q, 0.0))
            key = (st, -prio[i], i)
            if best is None or key < best[0]:
                best = (key, i, st)
        _, i, st = best
        ready.remove(i)
        q = ops[i]["q"]
        free[q] = st + ops[i]["cost"]
        fin[i] = st + ops[i]["cost"] + ops[i]["lat"]
        order.append((i, st))
        for j in succ[i]:
            ready_at[j] = max(ready_at[j], fin[i] + (WAKE if ops[j]["q"] != q else 20))
            left[j] -= 1
            if left[j] == 0:
                ready.append(j)
    return order, max(fin)


CACHE = {}


def plan():
    if "order" not in CACHE:
        CACHE["ops"] = build()
        CACHE["order"], CACHE["span"] = schedule(CACHE["ops"])
    return CACHE["ops"], [i for (i, st) in CACHE["order"]]


def rank_program(g, core, T, topo):
    rank = T.rank_of(core)
    if rank is None:
        return
    ops, order = plan()
    sent = [0]

    def to(dst, out, a, b, src, sem):
        rid, pid, _se = topo.addr(dst)
        sent[0] += len(topo.engines(core, dst))
        g.remote_dma(out_ap=T[out][:, a:b], in_ap=T[src][:, a:b], remote_sem=T.sem[sem], local_sem=T.sem.sent, pid=pid, routing_id=rid,
                     dma_engine_mask=topo.mask(core, dst))
        return []
    X = {"send": lambda t, *r: to(T.cores[(rank + 1 + t) % NR], *r), "back": lambda t, *r: to(T.cores[(rank - 1 - t) % NR], *r)}
    src = {"x": lambda s: T.cores[(rank - 1 - int(s[2])) % NR], "f": lambda s: T.cores[(rank - 1 - int(s[2])) % NR],
           "r": lambda s: T.cores[(rank + 1 + int(s[2])) % NR], "e": lambda s: T.cores[(rank + 2) % NR]}
    queues = {"v": g.vector, "s": g.scalar, "p": g.tensor, "g": g, "y": g.sync}
    count = {q: 0 for q in COUNTER}
    known = {q: {} for q in queues}
    clock, at, total = {}, {}, {}
    for i in order:
        o = ops[i]
        q, sem = o["q"], o["sem"]
        if q == "r":
            k = len(topo.engines(src[sem[1]](sem), core))
            at[i], clock[i], total[sem] = (sem, k), {sem: k}, k
            continue
        kn = known[q]
        need = sorted([d for d in o["deps"] if at.get(d) is not None and not (q == "p" and ops[d]["q"] == "p")], key=lambda d: -d)
        for d in need:
            s, v = at[d]
            if kn.get(s, 0) < v:
                same = [e for e in need if at[e][0] == s]
                queues[q].wait_ge(T.sem[s], max([at[e][1] for e in same]))
                for e in same:
                    for k2, v2 in clock[e].items():
                        kn[k2] = max(kn.get(k2, 0), v2)
        ins = o["emit"](g, T, X)
        c = dict(kn)
        at[i] = None
        if sem is not None:
            ins[0].then_inc(T.sem[sem], 16)
            at[i] = (sem, 16)
        elif o["n"]:
            ins[0].then_inc(T.sem[COUNTER[q]], 1)
            count[q] += 1
            at[i] = (COUNTER[q], count[q])
        if at[i] is not None:
            c[at[i][0]] = total[at[i][0]] = at[i][1]
        clock[i] = c
    total["sent"] = sent[0]
    for s in total:
        g.wait_ge(T.sem[s], total[s])
